import numpy as np, ml_dtypes
CORES = [61,69,101,62,70,102]
N = 6
DEG, TK, TIMES = 3, 128, 2
MASK = [[5,0,1],[0,1,2],[1,2,3],[2,3,4],[3,4,5],[4,5,0]]
def setup_inputs(rng):
    return {"x": rng.standard_normal((N, 128, TK), dtype=np.float32).astype(ml_dtypes.bfloat16), "w": (rng.standard_normal((N, 128, DEG * 128), dtype=np.float32) / np.float32(np.sqrt(128 * DEG / 2))).astype(ml_dtypes.bfloat16)}
def setup_inputs_big(rng):
    d = setup_inputs(rng)
    for k in ("x",): d[k] = (d[k].astype(np.float32) * 1048576.0).astype(d[k].dtype)
    return d
def setup_inputs_small(rng):
    d = setup_inputs(rng)
    for k in ("x",): d[k] = (d[k].astype(np.float32) * (1 / 1048576.0)).astype(d[k].dtype)
    return d
def setup_inputs_apart(rng):
    d = setup_inputs(rng)
    f = (10.0 ** rng.permutation(np.linspace(-1.5, 1.5, N))).astype(np.float32).reshape(N, 1, 1)
    for k in ("x",): d[k] = (d[k].astype(np.float32) * f).astype(d[k].dtype)
    return d
def reference(x, w):
    X, W = x.astype(np.float64), w.astype(np.float64)
    h = list(X)
    for _ in range(TIMES):
        h = [sum(W[r][:, 128 * i:128 * i + 128].T @ h[j] for i, j in enumerate(MASK[r])) for r in range(N)]
    return {"y": np.stack(h).astype(ml_dtypes.bfloat16)}

@@ -1,0 +1,180 @@
+from concourse.bass import DstId, RemoteDMATransfer
+
+NR, TK, DEG = 6, 128, 3
+
+SCRATCH = {
+    "xs": ("sbuf", [128, NR * TK], "bfloat16"),
+    "hs": ("sbuf", [128, NR * TK], "bfloat16"),
+    "wo": ("sbuf", [128, DEG * TK], "bfloat16"),
+    "wg": ("sbuf", [128, DEG * TK], "bfloat16"),
+    "yo": ("sbuf", [128, TK], "bfloat16"),
+    "p0": ("psum", [128, 512], "float32"),
+    "p1": ("psum", [128, 512], "float32"),
+    "py": ("psum", [128, 512], "float32"),
+}
+SEMAPHORES = (["xl", "wl", "wa", "sent", "st", "my", "cy"]
+              + ["xa%d" % j for j in range(NR)] + ["ha%d" % j for j in range(NR)]
+              + ["mh%d" % j for j in range(NR)] + ["ch%d" % j for j in range(NR)])
+
+
+def _uniq(seq):
+    out = []
+    for v in seq:
+        if v not in out:
+            out.append(v)
+    return out
+
+
+def _plan(T, topo):
+    cores, mask = list(T.cores), T.tables["MASK"]
+    n = len(cores)
+    readers = [[q for q in range(n) if j in mask[q]] for j in range(n)]
+    site = []
+    for j in range(n):
+        c = cores[j]
+        need = [cores[q] for q in readers[j] if q != j]
+        if all(topo.may_write(c, d) for d in need):
+            site.append(c)
+        else:
+            site.append([d for d in cores if d != c and topo.chip(d) == topo.chip(c) and topo.die(d) == topo.die(c)
+                         and all(topo.may_write(d, t) for t in need if t != d)][0])
+    direct, relayed = [], []
+    for j in range(n):
+        tg = [t for t in _uniq(site[q] for q in readers[j]) if t != cores[j]]
+        direct.append([t for t in tg if topo.may_write(cores[j], t)])
+        relayed.append([t for t in tg if not topo.may_write(cores[j], t)])
+
+    def depth(j, t):
+        return 0 if t == cores[j] else (1 if t in direct[j] else 2)
+
+    late = [max(depth(j, site[q]) for j in mask[q]) for q in range(n)]
+    return cores, mask, readers, site, direct, relayed, depth, late
+
+
+def rank_program(g, core, T, topo):
+    cores, mask, readers, site, direct, relayed, depth, late = _plan(T, topo)
+    n = len(cores)
+    rank = T.rank_of(core)
+    hosted = [q for q in range(n) if site[q] == core]
+    if rank is None and not hosted:
+        return
+    sem = T.sem
+
+    def slot(buf, j):
+        return buf[:, j * TK:(j + 1) * TK]
+
+    def bits(m):
+        return [b for b in range(m.bit_length()) if (m >> b) & 1]
+
+    def engines(src, dst):
+        allowed = bits(topo.mask(src, dst))
+        if topo.chip(src) != topo.chip(dst):
+            return allowed
+        away = [d for d in cores if topo.chip(d) != topo.chip(src)][0]
+        off = bits(topo.mask(src, away))
+        return [b for b in allowed if b not in off]
+
+    def count(src, dst):
+        return len(engines(src, dst))
+
+    sent = [0]
+
+    def send(src_ap, dst_ap, dsts, rsem):
+        eng = engines(core, dsts[0])
+        ids = [DstId(rid=topo.addr(d)[0], pnc=topo.addr(d)[1]) for d in dsts]
+        g.remote_dma_fused([RemoteDMATransfer(dst_ids=ids, dma_engine_mask=sum(1 << b for b in eng), remote_sem=rsem,
+                                              srcs=[src_ap], dsts=[dst_ap for _ in dsts], alu_op=0)],
+                           local_sem=sem.sent)
+        sent[0] += len(eng)
+
+    if rank is not None:
+        g.sync.dma_start(slot(T.xs, rank), T.x[:, :]).then_inc(sem.xl, 16)
+        g.scalar.dma_start(T.wo[:, :], T.w[:, :]).then_inc(sem.wl, 16)
+
+    order = sorted(hosted, key=lambda q: (late[q], 0 if q != rank else 1))
+    guests = [q for q in hosted if q != rank]
+
+    if rank is not None:
+        g.wait_ge(sem.xl, 16)
+        s = site[rank]
+        if s != core:
+            send(slot(T.xs, rank), slot(T.xs, rank), [s], sem["xa%d" % rank])
+            g.wait_ge(sem.wl, 16)
+            send(T.wo[:, :], T.wg[:, :], [s], sem.wa)
+            rest = [t for t in direct[rank] if t != s]
+        else:
+            rest = direct[rank]
+        if rest:
+            send(slot(T.xs, rank), slot(T.xs, rank), rest, sem["xa%d" % rank])
+    for j in guests:
+        if relayed[j]:
+            g.wait_ge(sem["xa%d" % j], count(cores[j], core))
+            send(slot(T.xs, j), slot(T.xs, j), relayed[j], sem["xa%d" % j])
+    held = []
+    for q in order:
+        fin = [cores[r] for r in readers[q] if cores[r] != core]
+        off = [d for d in fin if topo.chip(d) != topo.chip(core)]
+        on = [d for d in fin if topo.chip(d) == topo.chip(core)]
+        g.wait_ge(sem["ch%d" % q], 1)
+        if off:
+            send(slot(T.hs, q), slot(T.hs, q), off, sem["ha%d" % q])
+        if on:
+            held.append((q, on))
+    for q, on in held:
+        send(slot(T.hs, q), slot(T.hs, q), on, sem["ha%d" % q])
+
+    seen = {}
+
+    def twait(s, name, val):
+        if name not in seen:
+            seen[name] = 1
+            g.tensor.wait_ge(s, val)
+
+    bank = {}
+    for k, q in enumerate(order):
+        bank[q] = T["p%d" % k]
+    jobs = sorted([(late[q], depth(j, core), 0 if q == rank else 1, q, i, j) for q in hosted for i, j in enumerate(mask[q])])
+    done = {}
+    for _, _, _, q, i, j in jobs:
+        if cores[j] == core:
+            twait(sem.xl, "xl", 16)
+        else:
+            src = cores[j] if core in direct[j] else site[j]
+            twait(sem["xa%d" % j], "xa%d" % j, count(src, core))
+        if q == rank:
+            twait(sem.wl, "wl", 16)
+            w = T.wo
+        else:
+            twait(sem.wa, "wa", count(cores[q], core))
+            w = T.wg
+        done[q] = done.get(q, 0) + 1
+        mm = g.tensor.matmul(bank[q][:, 0:TK], slot(w, i), slot(T.xs, j), done[q] == 1, done[q] == len(mask[q]))
+        if done[q] == len(mask[q]):
+            mm.then_inc(sem["mh%d" % q], 1)
+
+    for q in order:
+        g.vector.wait_ge(sem["mh%d" % q], 1)
+        g.vector.tensor_copy(slot(T.hs, q), bank[q][:, 0:TK]).then_inc(sem["ch%d" % q], 1)
+
+    if rank is not None:
+        def when(j):
+            rivals = [q for q in range(n) if site[q] == site[j] and late[q] == late[j]]
+            pos = sorted(rivals, key=lambda q: 0 if cores[q] != site[q] else 1).index(j)
+            return (0 if site[j] == core else 1, late[j], pos)
+        fj = sorted([(when(j), i, j) for i, j in enumerate(mask[rank])])
+        twait(sem.wl, "wl", 16)
+        for k, (_, i, j) in enumerate(fj):
+            if site[j] == core:
+                g.tensor.wait_ge(sem["ch%d" % j], 1)
+            else:
+                g.tensor.wait_ge(sem["ha%d" % j], count(site[j], core))
+            mm = g.tensor.matmul(T.py[:, 0:TK], slot(T.wo, i), slot(T.hs, j), k == 0, k == len(fj) - 1)
+        mm.then_inc(sem.my, 1)
+        g.vector.wait_ge(sem.my, 1)
+        g.vector.tensor_copy(T.yo[:, :], T.py[:, 0:TK]).then_inc(sem.cy, 1)
+        g.sync.wait_ge(sem.cy, 1)
+        g.sync.dma_start(T.y[:, :], T.yo[:, :]).then_inc(sem.st, 16)
+        g.sync.wait_ge(sem.st, 16)
+
+    if sent[0]:
+        g.wait_ge(sem.sent, sent[0])

@@ -1,18 +1,24 @@
 from concourse.bass import DstId, RemoteDMATransfer
+from concourse.mybir import ActivationFunctionType
 
 NR, TK, DEG = 6, 128, 3
+HOPN = 4
 
 SCRATCH = {
     "xs": ("sbuf", [128, NR * TK], "bfloat16"),
-    "hs": ("sbuf", [128, NR * TK], "bfloat16"),
+    "hs": ("sbuf", [128, (NR + 1) * TK], "bfloat16"),
     "wo": ("sbuf", [128, DEG * TK], "bfloat16"),
     "wg": ("sbuf", [128, DEG * TK], "bfloat16"),
+    "wq": ("sbuf", [128, TK], "bfloat16"),
     "yo": ("sbuf", [128, TK], "bfloat16"),
+    "xd": ("dram", [128, TK], "bfloat16"),
+    "xg": ("dram", [128, TK], "bfloat16"),
     "p0": ("psum", [128, 512], "float32"),
     "p1": ("psum", [128, 512], "float32"),
+    "p2": ("psum", [128, 512], "float32"),
     "py": ("psum", [128, 512], "float32"),
 }
-SEMAPHORES = (["xl", "wl", "wa", "sent", "st", "my", "cy"]
+SEMAPHORES = (["dl", "xr", "xl", "wl", "wa", "sent", "st", "my", "cy", "wqa", "mq", "cq", "qa"]
               + ["xa%d" % j for j in range(NR)] + ["ha%d" % j for j in range(NR)]
               + ["mh%d" % j for j in range(NR)] + ["ch%d" % j for j in range(NR)])
 
@@ -48,17 +54,29 @@ def _plan(T, topo):
         return 0 if t == cores[j] else (1 if t in direct[j] else 2)
 
     late = [max(depth(j, site[q]) for j in mask[q]) for q in range(n)]
-    return cores, mask, readers, site, direct, relayed, depth, late
+    cut = {}
+    for sc in _uniq(site):
+        lq = [q for q in range(n) if site[q] == sc and late[q] == 2]
+        for q in lq:
+            far = [(i, j) for i, j in enumerate(mask[q]) if depth(j, sc) == 2]
+            if len(lq) > 1 and cores[q] == sc and len(far) == 1 and not cut:
+                j = far[0][1]
+                if all(topo.may_write(cores[j], cores[r]) for r in readers[q] if r not in (q, j)) and j in readers[q]:
+                    cut[q] = far[0]
+    for q in cut:
+        late[q] = 1
+    return cores, mask, readers, site, direct, relayed, depth, late, cut
 
 
 def rank_program(g, core, T, topo):
-    cores, mask, readers, site, direct, relayed, depth, late = _plan(T, topo)
+    cores, mask, readers, site, direct, relayed, depth, late, cut = _plan(T, topo)
     n = len(cores)
     rank = T.rank_of(core)
     hosted = [q for q in range(n) if site[q] == core]
     if rank is None and not hosted:
         return
     sem = T.sem
+    helps = [q for q in cut if cores[cut[q][1]] == core]
 
     def slot(buf, j):
         return buf[:, j * TK:(j + 1) * TK]
@@ -79,49 +97,76 @@ def rank_program(g, core, T, topo):
 
     sent = [0]
 
-    def send(src_ap, dst_ap, dsts, rsem):
+    def send(src_ap, dst_ap, dsts, rsem, k=None):
         eng = engines(core, dsts[0])
+        eng = eng if k is None else eng[:k]
         ids = [DstId(rid=topo.addr(d)[0], pnc=topo.addr(d)[1]) for d in dsts]
         g.remote_dma_fused([RemoteDMATransfer(dst_ids=ids, dma_engine_mask=sum(1 << b for b in eng), remote_sem=rsem,
                                               srcs=[src_ap], dsts=[dst_ap for _ in dsts], alu_op=0)],
                            local_sem=sem.sent)
         sent[0] += len(eng)
 
+    def same(a, b):
+        return topo.chip(a) == topo.chip(b)
+
+    def due(j, t):
+        return min(late[q] for q in readers[j] if site[q] == t)
+
+    def xkey(j, t):
+        return 0.0 if cores[j] == t else (3.0 if t in relayed[j] else (1.0 if same(cores[j], t) else 2.0))
+
+    def horder(sc):
+        return sorted([q for q in range(n) if site[q] == sc], key=lambda q: (late[q], 0 if cores[q] != sc else 1))
+
+    def part(q):
+        return NR if q in cut else q
+
     if rank is not None:
-        g.sync.dma_start(slot(T.xs, rank), T.x[:, :]).then_inc(sem.xl, 16)
+        g.sync.dma_start(T.xd[:, :], T.x[:, :]).then_inc(sem.dl, 16)
+        if any(rank in mask[q] for q in hosted) or helps:
+            g.sync.dma_start(slot(T.xs, rank), T.x[:, :]).then_inc(sem.xl, 16)
         g.scalar.dma_start(T.wo[:, :], T.w[:, :]).then_inc(sem.wl, 16)
 
-    order = sorted(hosted, key=lambda q: (late[q], 0 if q != rank else 1))
+    order = horder(core)
     guests = [q for q in hosted if q != rank]
 
     if rank is not None:
-        g.wait_ge(sem.xl, 16)
+        g.wait_ge(sem.dl, 16)
         s = site[rank]
+        if s != core and relayed[rank]:
+            send(T.xd[:, :], T.xg[:, :], [s], sem.xr, HOPN)
+        todo = sorted(direct[rank], key=lambda t: (due(rank, t), 0 if not same(t, core) else 1))
+        while todo:
+            grp = [t for t in todo if same(t, core) == same(todo[0], core)]
+            send(T.xd[:, :], slot(T.xs, rank), grp, sem["xa%d" % rank])
+            todo = [t for t in todo if t not in grp]
         if s != core:
-            send(slot(T.xs, rank), slot(T.xs, rank), [s], sem["xa%d" % rank])
             g.wait_ge(sem.wl, 16)
             send(T.wo[:, :], T.wg[:, :], [s], sem.wa)
-            rest = [t for t in direct[rank] if t != s]
-        else:
-            rest = direct[rank]
-        if rest:
-            send(slot(T.xs, rank), slot(T.xs, rank), rest, sem["xa%d" % rank])
+        if rank in cut:
+            g.wait_ge(sem.wl, 16)
+            send(slot(T.wo, cut[rank][0]), T.wq[:, :], [cores[cut[rank][1]]], sem.wqa)
     for j in guests:
         if relayed[j]:
-            g.wait_ge(sem["xa%d" % j], count(cores[j], core))
-            send(slot(T.xs, j), slot(T.xs, j), relayed[j], sem["xa%d" % j])
+            g.wait_ge(sem.xr, HOPN)
+            send(T.xg[:, :], slot(T.xs, j), relayed[j], sem["xa%d" % j])
+    for q in helps:
+        fin = [cores[r] for r in readers[q] if cores[r] not in (core, site[q])]
+        g.wait_ge(sem.cq, 1)
+        if fin:
+            send(slot(T.hs, q), slot(T.hs, q), fin, sem.qa)
     held = []
     for q in order:
         fin = [cores[r] for r in readers[q] if cores[r] != core]
-        off = [d for d in fin if topo.chip(d) != topo.chip(core)]
-        on = [d for d in fin if topo.chip(d) == topo.chip(core)]
+        off = [d for d in fin if not same(d, core)]
+        on = [d for d in fin if same(d, core)]
         g.wait_ge(sem["ch%d" % q], 1)
         if off:
-            send(slot(T.hs, q), slot(T.hs, q), off, sem["ha%d" % q])
+            send(slot(T.hs, part(q)), slot(T.hs, part(q)), off, sem["ha%d" % q])
         if on:
             held.append((q, on))
     for q, on in held:
-        send(slot(T.hs, q), slot(T.hs, q), on, sem["ha%d" % q])
+        send(slot(T.hs, part(q)), slot(T.hs, part(q)), on, sem["ha%d" % q])
 
     seen = {}
 
@@ -130,45 +175,64 @@ def rank_program(g, core, T, topo):
             seen[name] = 1
             g.tensor.wait_ge(s, val)
 
-    bank = {}
-    for k, q in enumerate(order):
-        bank[q] = T["p%d" % k]
-    jobs = sorted([(late[q], depth(j, core), 0 if q == rank else 1, q, i, j) for q in hosted for i, j in enumerate(mask[q])])
-    done = {}
-    for _, _, _, q, i, j in jobs:
+    def xwait(j):
         if cores[j] == core:
             twait(sem.xl, "xl", 16)
         else:
             src = cores[j] if core in direct[j] else site[j]
             twait(sem["xa%d" % j], "xa%d" % j, count(src, core))
+
+    bank = {}
+    for k, q in enumerate(order):
+        bank[q] = T["p%d" % k]
+    for q in helps:
+        xwait(cut[q][1])
+        twait(sem.wqa, "wqa", count(site[q], core))
+        g.tensor.matmul(T.p2[:, 0:TK], T.wq[:, :], slot(T.xs, cut[q][1]), True, True).then_inc(sem.mq, 1)
+    jobs = sorted([(max(xkey(j, core), 0.0 if q == rank else 2.5), 1 if (q in cut and cut[q] == (i, j)) else 0,
+                    order.index(q), i, q, j) for q in hosted for i, j in enumerate(mask[q])])
+    done = {}
+    for _, apart, _, i, q, j in jobs:
+        xwait(j)
         if q == rank:
             twait(sem.wl, "wl", 16)
             w = T.wo
         else:
             twait(sem.wa, "wa", count(cores[q], core))
             w = T.wg
+        if apart:
+            g.tensor.matmul(T.p2[:, 0:TK], slot(w, i), slot(T.xs, j), True, True).then_inc(sem.mq, 1)
+            continue
+        terms = len(mask[q]) - (1 if q in cut else 0)
         done[q] = done.get(q, 0) + 1
-        mm = g.tensor.matmul(bank[q][:, 0:TK], slot(w, i), slot(T.xs, j), done[q] == 1, done[q] == len(mask[q]))
-        if done[q] == len(mask[q]):
+        mm = g.tensor.matmul(bank[q][:, 0:TK], slot(w, i), slot(T.xs, j), done[q] == 1, done[q] == terms)
+        if done[q] == terms:
             mm.then_inc(sem["mh%d" % q], 1)
 
     for q in order:
         g.vector.wait_ge(sem["mh%d" % q], 1)
-        g.vector.tensor_copy(slot(T.hs, q), bank[q][:, 0:TK]).then_inc(sem["ch%d" % q], 1)
+        g.vector.tensor_copy(slot(T.hs, part(q)), bank[q][:, 0:TK]).then_inc(sem["ch%d" % q], 1)
+    for q in cut:
+        if q in helps or q in hosted:
+            g.scalar.wait_ge(sem.mq, 1)
+            g.scalar.activation(slot(T.hs, q), T.p2[:, 0:TK], ActivationFunctionType.Copy).then_inc(sem.cq, 1)
 
     if rank is not None:
-        def when(j):
-            rivals = [q for q in range(n) if site[q] == site[j] and late[q] == late[j]]
-            pos = sorted(rivals, key=lambda q: 0 if cores[q] != site[q] else 1).index(j)
-            return (0 if site[j] == core else 1, late[j], pos)
-        fj = sorted([(when(j), i, j) for i, j in enumerate(mask[rank])])
+        fj = []
+        for i, j in enumerate(mask[rank]):
+            here = site[j] == core
+            pos = horder(site[j]).index(j)
+            fj.append((late[j] + (0.0 if here else 1.0), pos, i, part(j),
+                       "ch%d" % j if here else "ha%d" % j, 1 if here else count(site[j], core)))
+            if j in cut:
+                mine = here or j in helps
+                fj.append((2.0 if here else (1.5 if mine else 2.5), 0, i, j,
+                           "cq" if mine else "qa", 1 if mine else count(cores[cut[j][1]], core)))
+        fj.sort()
         twait(sem.wl, "wl", 16)
-        for k, (_, i, j) in enumerate(fj):
-            if site[j] == core:
-                g.tensor.wait_ge(sem["ch%d" % j], 1)
-            else:
-                g.tensor.wait_ge(sem["ha%d" % j], count(site[j], core))
-            mm = g.tensor.matmul(T.py[:, 0:TK], slot(T.wo, i), slot(T.hs, j), k == 0, k == len(fj) - 1)
+        for k, (_, _, i, sl, name, val) in enumerate(fj):
+            g.tensor.wait_ge(sem[name], val)
+            mm = g.tensor.matmul(T.py[:, 0:TK], slot(T.wo, i), slot(T.hs, sl), k == 0, k == len(fj) - 1)
         mm.then_inc(sem.my, 1)
         g.vector.wait_ge(sem.my, 1)
         g.vector.tensor_copy(T.yo[:, :], T.py[:, 0:TK]).then_inc(sem.cy, 1)

from concourse.bass import DstId, RemoteDMATransfer
from concourse.mybir import ActivationFunctionType

NR, TK, DEG = 6, 128, 3
HOPN = 4

SCRATCH = {
    "xs": ("sbuf", [128, NR * TK], "bfloat16"),
    "hs": ("sbuf", [128, (NR + 1) * TK], "bfloat16"),
    "wo": ("sbuf", [128, DEG * TK], "bfloat16"),
    "wg": ("sbuf", [128, DEG * TK], "bfloat16"),
    "wq": ("sbuf", [128, TK], "bfloat16"),
    "yo": ("sbuf", [128, TK], "bfloat16"),
    "xd": ("dram", [128, TK], "bfloat16"),
    "xg": ("dram", [128, TK], "bfloat16"),
    "p0": ("psum", [128, 512], "float32"),
    "p1": ("psum", [128, 512], "float32"),
    "p2": ("psum", [128, 512], "float32"),
    "py": ("psum", [128, 512], "float32"),
}
SEMAPHORES = (["dl", "xr", "xl", "wl", "wa", "sent", "st", "my", "cy", "wqa", "mq", "cq", "qa"]
              + ["xa%d" % j for j in range(NR)] + ["ha%d" % j for j in range(NR)]
              + ["mh%d" % j for j in range(NR)] + ["ch%d" % j for j in range(NR)])


def _uniq(seq):
    out = []
    for v in seq:
        if v not in out:
            out.append(v)
    return out


def _plan(T, topo):
    cores, mask = list(T.cores), T.tables["MASK"]
    n = len(cores)
    readers = [[q for q in range(n) if j in mask[q]] for j in range(n)]
    site = []
    for j in range(n):
        c = cores[j]
        need = [cores[q] for q in readers[j] if q != j]
        if all(topo.may_write(c, d) for d in need):
            site.append(c)
        else:
            site.append([d for d in cores if d != c and topo.chip(d) == topo.chip(c) and topo.die(d) == topo.die(c)
                         and all(topo.may_write(d, t) for t in need if t != d)][0])
    direct, relayed = [], []
    for j in range(n):
        tg = [t for t in _uniq(site[q] for q in readers[j]) if t != cores[j]]
        direct.append([t for t in tg if topo.may_write(cores[j], t)])
        relayed.append([t for t in tg if not topo.may_write(cores[j], t)])

    def depth(j, t):
        return 0 if t == cores[j] else (1 if t in direct[j] else 2)

    late = [max(depth(j, site[q]) for j in mask[q]) for q in range(n)]
    cut = {}
    for sc in _uniq(site):
        lq = [q for q in range(n) if site[q] == sc and late[q] == 2]
        for q in lq:
            far = [(i, j) for i, j in enumerate(mask[q]) if depth(j, sc) == 2]
            if len(lq) > 1 and cores[q] == sc and len(far) == 1 and not cut:
                j = far[0][1]
                if all(topo.may_write(cores[j], cores[r]) for r in readers[q] if r not in (q, j)) and j in readers[q]:
                    cut[q] = far[0]
    for q in cut:
        late[q] = 1
    return cores, mask, readers, site, direct, relayed, depth, late, cut


def rank_program(g, core, T, topo):
    cores, mask, readers, site, direct, relayed, depth, late, cut = _plan(T, topo)
    n = len(cores)
    rank = T.rank_of(core)
    hosted = [q for q in range(n) if site[q] == core]
    if rank is None and not hosted:
        return
    sem = T.sem
    helps = [q for q in cut if cores[cut[q][1]] == core]

    def slot(buf, j):
        return buf[:, j * TK:(j + 1) * TK]

    def bits(m):
        return [b for b in range(m.bit_length()) if (m >> b) & 1]

    def engines(src, dst):
        allowed = bits(topo.mask(src, dst))
        if topo.chip(src) != topo.chip(dst):
            return allowed
        away = [d for d in cores if topo.chip(d) != topo.chip(src)][0]
        off = bits(topo.mask(src, away))
        return [b for b in allowed if b not in off]

    def count(src, dst):
        return len(engines(src, dst))

    sent = [0]

    def send(src_ap, dst_ap, dsts, rsem, k=None):
        eng = engines(core, dsts[0])
        eng = eng if k is None else eng[:k]
        ids = [DstId(rid=topo.addr(d)[0], pnc=topo.addr(d)[1]) for d in dsts]
        g.remote_dma_fused([RemoteDMATransfer(dst_ids=ids, dma_engine_mask=sum(1 << b for b in eng), remote_sem=rsem,
                                              srcs=[src_ap], dsts=[dst_ap for _ in dsts], alu_op=0)],
                           local_sem=sem.sent)
        sent[0] += len(eng)

    def same(a, b):
        return topo.chip(a) == topo.chip(b)

    def due(j, t):
        return min(late[q] for q in readers[j] if site[q] == t)

    def xkey(j, t):
        return 0.0 if cores[j] == t else (3.0 if t in relayed[j] else (1.0 if same(cores[j], t) else 2.0))

    def horder(sc):
        return sorted([q for q in range(n) if site[q] == sc], key=lambda q: (late[q], 0 if cores[q] != sc else 1))

    def part(q):
        return NR if q in cut else q

    if rank is not None:
        g.sync.dma_start(T.xd[:, :], T.x[:, :]).then_inc(sem.dl, 16)
        if any(rank in mask[q] for q in hosted) or helps:
            g.sync.dma_start(slot(T.xs, rank), T.x[:, :]).then_inc(sem.xl, 16)
        g.scalar.dma_start(T.wo[:, :], T.w[:, :]).then_inc(sem.wl, 16)

    order = horder(core)
    guests = [q for q in hosted if q != rank]

    if rank is not None:
        g.wait_ge(sem.dl, 16)
        s = site[rank]
        if s != core and relayed[rank]:
            send(T.xd[:, :], T.xg[:, :], [s], sem.xr, HOPN)
        todo = sorted(direct[rank], key=lambda t: (due(rank, t), 0 if not same(t, core) else 1))
        while todo:
            grp = [t for t in todo if same(t, core) == same(todo[0], core)]
            send(T.xd[:, :], slot(T.xs, rank), grp, sem["xa%d" % rank])
            todo = [t for t in todo if t not in grp]
        if s != core:
            g.wait_ge(sem.wl, 16)
            send(T.wo[:, :], T.wg[:, :], [s], sem.wa)
        if rank in cut:
            g.wait_ge(sem.wl, 16)
            send(slot(T.wo, cut[rank][0]), T.wq[:, :], [cores[cut[rank][1]]], sem.wqa)
    for j in guests:
        if relayed[j]:
            g.wait_ge(sem.xr, HOPN)
            send(T.xg[:, :], slot(T.xs, j), relayed[j], sem["xa%d" % j])
    for q in helps:
        fin = [cores[r] for r in readers[q] if cores[r] not in (core, site[q])]
        g.wait_ge(sem.cq, 1)
        if fin:
            send(slot(T.hs, q), slot(T.hs, q), fin, sem.qa)
    held = []
    for q in order:
        fin = [cores[r] for r in readers[q] if cores[r] != core]
        off = [d for d in fin if not same(d, core)]
        on = [d for d in fin if same(d, core)]
        g.wait_ge(sem["ch%d" % q], 1)
        if off:
            send(slot(T.hs, part(q)), slot(T.hs, part(q)), off, sem["ha%d" % q])
        if on:
            held.append((q, on))
    for q, on in held:
        send(slot(T.hs, part(q)), slot(T.hs, part(q)), on, sem["ha%d" % q])

    seen = {}

    def twait(s, name, val):
        if name not in seen:
            seen[name] = 1
            g.tensor.wait_ge(s, val)

    def xwait(j):
        if cores[j] == core:
            twait(sem.xl, "xl", 16)
        else:
            src = cores[j] if core in direct[j] else site[j]
            twait(sem["xa%d" % j], "xa%d" % j, count(src, core))

    bank = {}
    for k, q in enumerate(order):
        bank[q] = T["p%d" % k]
    for q in helps:
        xwait(cut[q][1])
        twait(sem.wqa, "wqa", count(site[q], core))
        g.tensor.matmul(T.p2[:, 0:TK], T.wq[:, :], slot(T.xs, cut[q][1]), True, True).then_inc(sem.mq, 1)
    jobs = sorted([(max(xkey(j, core), 0.0 if q == rank else 2.5), 1 if (q in cut and cut[q] == (i, j)) else 0,
                    order.index(q), i, q, j) for q in hosted for i, j in enumerate(mask[q])])
    done = {}
    for _, apart, _, i, q, j in jobs:
        xwait(j)
        if q == rank:
            twait(sem.wl, "wl", 16)
            w = T.wo
        else:
            twait(sem.wa, "wa", count(cores[q], core))
            w = T.wg
        if apart:
            g.tensor.matmul(T.p2[:, 0:TK], slot(w, i), slot(T.xs, j), True, True).then_inc(sem.mq, 1)
            continue
        terms = len(mask[q]) - (1 if q in cut else 0)
        done[q] = done.get(q, 0) + 1
        mm = g.tensor.matmul(bank[q][:, 0:TK], slot(w, i), slot(T.xs, j), done[q] == 1, done[q] == terms)
        if done[q] == terms:
            mm.then_inc(sem["mh%d" % q], 1)

    for q in order:
        g.vector.wait_ge(sem["mh%d" % q], 1)
        g.vector.tensor_copy(slot(T.hs, part(q)), bank[q][:, 0:TK]).then_inc(sem["ch%d" % q], 1)
    for q in cut:
        if q in helps or q in hosted:
            g.scalar.wait_ge(sem.mq, 1)
            g.scalar.activation(slot(T.hs, q), T.p2[:, 0:TK], ActivationFunctionType.Copy).then_inc(sem.cq, 1)

    if rank is not None:
        fj = []
        for i, j in enumerate(mask[rank]):
            here = site[j] == core
            pos = horder(site[j]).index(j)
            fj.append((late[j] + (0.0 if here else 1.0), pos, i, part(j),
                       "ch%d" % j if here else "ha%d" % j, 1 if here else count(site[j], core)))
            if j in cut:
                mine = here or j in helps
                fj.append((2.0 if here else (1.5 if mine else 2.5), 0, i, j,
                           "cq" if mine else "qa", 1 if mine else count(cores[cut[j][1]], core)))
        fj.sort()
        twait(sem.wl, "wl", 16)
        for k, (_, _, i, sl, name, val) in enumerate(fj):
            g.tensor.wait_ge(sem[name], val)
            mm = g.tensor.matmul(T.py[:, 0:TK], slot(T.wo, i), slot(T.hs, sl), k == 0, k == len(fj) - 1)
        mm.then_inc(sem.my, 1)
        g.vector.wait_ge(sem.my, 1)
        g.vector.tensor_copy(T.yo[:, :], T.py[:, 0:TK]).then_inc(sem.cy, 1)
        g.sync.wait_ge(sem.cy, 1)
        g.sync.dma_start(T.y[:, :], T.yo[:, :]).then_inc(sem.st, 16)
        g.sync.wait_ge(sem.st, 16)

    if sent[0]:
        g.wait_ge(sem.sent, sent[0])
